import numpy as np
import ml_dtypes


def mxq(x, axis, fmt="e4m3"):
    dtype, down = {"e4m3": (ml_dtypes.float8_e4m3fn, 7), "e5m2": (ml_dtypes.float8_e5m2, 14)}[fmt]
    v = np.moveaxis(np.asarray(x, np.float32).astype(ml_dtypes.bfloat16).astype(np.float64), axis, -1)
    blocks = v.reshape(v.shape[:-1] + (-1, 32))
    amax = np.abs(blocks).max(-1, keepdims=True)
    byte = np.maximum(np.where(amax > 0, np.frexp(amax)[1] - 1 + 127, 0) - down, 1)
    scale = np.exp2(byte - 127.0)
    codes = (blocks / scale).astype(np.float32).astype(dtype).astype(np.float64)
    return np.moveaxis((codes * scale).reshape(v.shape), -1, axis)


WIDE = False


def mx_kscale(k):
    if not WIDE:
        return np.ones(k)
    levels = np.array([10, -10, 5, -5, 0])
    if k % 512:
        return np.exp2(np.random.permutation(np.resize(levels, k // 32))).repeat(32)
    a = np.empty((k // 512, 16))
    for p in range(k // 512):
        a[p, :8] = np.random.permutation(np.resize(levels, 8))
        for g in range(8):
            far = levels[np.abs(levels - a[p, g]) >= 10]
            a[p, g + 8] = far[np.random.randint(len(far))]
    return np.exp2(a.ravel()).repeat(32)


def f64(x):
    return np.asarray(x).astype(np.float64)


def striped(idx):
    return np.tile(idx.reshape(-1, 16).T, (8, 1)).astype(np.uint16)


def unstriped(offs):
    return offs[:16].T.reshape(-1).astype(np.int64)


def striped8(idx):
    return np.concatenate([x.reshape(-1, 16).T for x in idx]).astype(np.uint16)


def runs(offs, k):
    lists = np.stack([offs[16 * r : 16 * r + 16].T.reshape(-1) for r in range(8)]).astype(np.int64)
    return lists[np.arange(k) % 512 // 64]


def pack_weight(w):
    k, n = w.shape
    w = f64(np.asarray(w, np.float32).astype(ml_dtypes.bfloat16)).reshape(k // 32, 32, n)
    amax = np.abs(w).max(1)
    byte = np.clip(np.where(amax > 0, np.frexp(amax)[1] - 1 + 127 - 7, 1), 1, 254)
    scaled = (w * np.exp2(127.0 - byte)[:, None, :]).reshape(k, n).astype(np.float32)
    words = np.ascontiguousarray(scaled.reshape(k // 512, 128, 4, n).transpose(0, 1, 3, 2)).astype(ml_dtypes.float8_e4m3fn).view(np.uint8)
    return words, np.ascontiguousarray(byte.astype(np.uint8).reshape(k // 512, 16, n))


def unpack_weight(words, scales):
    g, p, n, _ = words.shape
    vals = np.ascontiguousarray(words).view(ml_dtypes.float8_e4m3fn).astype(np.float64) * np.repeat(np.exp2(scales.astype(np.float64) - 127.0), 8, axis=1)[..., None]
    return vals.transpose(0, 1, 3, 2).reshape(g * 512, n)


K, T, S, V, H = 512, 2048, 512, 512, 512


def setup_inputs():
    n = np.random.standard_normal
    s = mx_kscale(K)[:, None]
    u = mx_kscale(S)
    packed_xT = pack_weight(n((K, T)) * s)
    return {
        "x_words": packed_xT[0],
        "x_scales": packed_xT[1],
        "w1": (n((K, H)) / np.sqrt(K) / s).astype(np.float32),
        "w2": (n((K, H)) / np.sqrt(K) / s).astype(np.float32),
        "ga": (np.random.uniform(0.5, 1.5, (H, 1)) * u[:, None]).astype(np.float32),
        "gb": (np.random.uniform(0.5, 1.5, (H, 1)) / u[:, None]).astype(np.float32),
        "offs": striped(np.random.permutation(T)[:S]),
        "two": striped(np.random.permutation(T)[:V]),
        "n1": striped8(np.stack([np.random.permutation(S) for _ in range(8)])),
        "n2": striped8(np.stack([np.random.permutation(S) for _ in range(8)])),
        "n3": striped8(np.stack([np.random.permutation(S) for _ in range(8)])),
        "n4": striped8(np.stack([np.random.permutation(V) for _ in range(8)])),
        "n5": striped8(np.stack([np.random.permutation(V) for _ in range(8)])),
        "n6": striped8(np.stack([np.random.permutation(V) for _ in range(8)])),
        "n7": striped8(np.stack([np.random.permutation(V) for _ in range(8)])),
    }


def reference(x_words, x_scales, w1, w2, ga, gb, offs, two, n1, n2, n3, n4, n5, n6, n7):
    xq = unpack_weight(x_words, x_scales)[:, unstriped(offs)]
    a = mxq(f64(w1), 0, "e4m3").T @ xq
    z = f64(ga) * (np.maximum(a, a[np.arange(H)[:, None], runs(n1, H)]) - (np.maximum(a[np.arange(H)[:, None], runs(n2, H)], a[np.arange(H)[:, None], runs(n3, H)])))
    x_two = unpack_weight(x_words, x_scales)[:, unstriped(two)]
    b = mxq(f64(w2), 0, "e4m3").T @ x_two
    z2 = f64(gb) * (0.75 * (b[np.arange(H)[:, None], runs(n4, H)] + b[np.arange(H)[:, None], runs(n5, H)]) - b)
    s = 0.0625 * ((mxq(z, 0, "e4m3").T @ mxq(z2, 0, "e4m3")))
    return np.maximum(s[np.arange(S)[:, None], runs(n6, S)], s[np.arange(S)[:, None], runs(n7, S)]) - (0.75 * s)

@@ -1,0 +1,215 @@
+from contextlib import ExitStack
+
+import concourse.mybir as mybir
+
+K, T, S, V, H = 512, 2048, 512, 512, 512
+FLOPS = 3 * 2 * 512 * 512 * 512
+
+F32 = mybir.dt.float32
+BF16 = mybir.dt.bfloat16
+I32 = mybir.dt.int32
+U32 = mybir.dt.uint32
+U16 = mybir.dt.uint16
+U8 = mybir.dt.uint8
+FP8X4 = mybir.dt.float8_e4m3fn_x4
+ALU = mybir.AluOpType
+COPY = mybir.ActivationFunctionType.Copy
+
+P = 128
+PACK = 4
+HALF = 256
+B_CHUNKS = ((0, 256), (256, 128), (384, 128))
+
+
+def looked_up(window, offsets, first, count):
+    return window[:].indirect(offsets[:, first // 16 : (first + count) // 16])
+
+
+def tile_picked_kqmixlapover_none_p_kernel(
+    tc, x_words, x_scales, w1, w2, ga, gb, offs, two, n1, n2, n3, n4, n5, n6, n7, out
+):
+    nc = tc.nc
+    with ExitStack() as ctx:
+        keep = ctx.enter_context(tc.tile_pool(name="keep", bufs=1))
+        psum = ctx.enter_context(tc.psum_pool(name="psum", bufs=1))
+
+        def load_list(name, src):
+            tile = keep.tile([P, S // 16], U16, name="list_" + name)
+            nc.sync.dma_start(tile[:], src)
+            return tile
+
+        def mx_tiles(name, width):
+            codes = keep.tile([P, width], U32, name=name + "_codes", align_bytes=64)
+            scales = keep.tile([P, width], U8, name=name + "_scales", align_bytes=64)
+            return codes, scales
+
+        def product(acc, lhs, lhs_cols, rhs, rhs_cols):
+            nc.tensor.matmul_mx(
+                out=acc,
+                lhsT=lhs[0][:, lhs_cols].bitcast(FP8X4),
+                lhsT_scale=lhs[1][:, lhs_cols],
+                rhs=rhs[0][:, rhs_cols].bitcast(FP8X4),
+                rhs_scale=rhs[1][:, rhs_cols],
+                start=True,
+                stop=True,
+            )
+
+        table_scales = keep.tile([P, T], U8, name="table_scales")
+        nc.vector.memset(table_scales[:].bitcast(I32), 0)
+        l_offs = load_list("offs", offs)
+        l_two = load_list("two", two)
+        for q in range(4):
+            nc.scalar.dma_start(
+                table_scales[32 * q : 32 * q + 4, :].bitcast(I32), x_scales[0, 4 * q : 4 * q + 4, :].bitcast(I32)
+            )
+        w1_rows = w1.rearrange("(p j) c -> p j c", j=PACK)
+        w1_raw = []
+        for h in range(2):
+            raw = keep.tile([P, PACK, HALF], F32, name="w1_raw%d" % h)
+            nc.sync.dma_start(raw[:], w1_rows[:, :, h * HALF : (h + 1) * HALF])
+            w1_raw.append(raw)
+        table_words = keep.tile([P, T], I32, name="table_words")
+        nc.sync.dma_start(table_words[:], x_words[0].rearrange("p n t -> p (n t)").bitcast(I32))
+        ga_t = keep.tile([P, PACK], F32, name="ga_t")
+        gb_t = keep.tile([P, PACK], F32, name="gb_t")
+        nc.sync.dma_start(ga_t[:], ga.rearrange("(p t) o -> p (t o)", t=PACK))
+        nc.sync.dma_start(gb_t[:], gb.rearrange("(p t) o -> p (t o)", t=PACK))
+        l1 = load_list("n1", n1)
+        l2 = load_list("n2", n2)
+        l3 = load_list("n3", n3)
+        w2_raw = keep.tile([P, PACK, H], F32, name="w2_raw")
+        nc.sync.dma_start(w2_raw[:], w2.rearrange("(p j) c -> p j c", j=PACK))
+        l4 = load_list("n4", n4)
+        l5 = load_list("n5", n5)
+        l6 = load_list("n6", n6)
+        l7 = load_list("n7", n7)
+
+        sign = keep.tile([P, PACK], F32, name="sign")
+        nonneg = keep.tile([P, PACK], F32, name="nonneg")
+        ga_abs = keep.tile([P, PACK], F32, name="ga_abs")
+        gb_one = keep.tile([P, PACK], F32, name="gb_one")
+        gb_34 = keep.tile([P, PACK], F32, name="gb_34")
+        nc.gpsimd.tensor_scalar(nonneg[:], ga_t[:], 0.0, 2.0, ALU.is_ge, ALU.mult)
+        nc.gpsimd.tensor_scalar(sign[:], nonneg[:], 1.0, -1.0, ALU.mult, ALU.add)
+        nc.gpsimd.tensor_tensor(ga_abs[:], ga_t[:], sign[:], ALU.mult)
+        nc.gpsimd.tensor_tensor(gb_one[:], gb_t[:], sign[:], ALU.mult)
+        nc.gpsimd.tensor_scalar(gb_34[:], gb_one[:], 0.75, 0.0, ALU.mult, ALU.add)
+
+        xa = mx_tiles("xa", S)
+        xb = mx_tiles("xb", V)
+        nc.vector.tensor_copy(xa[1][:], table_scales[:].indirect(l_offs[:]))
+        nc.vector.tensor_copy(xb[1][:], table_scales[:].indirect(l_two[:]))
+
+        w1_bf = keep.tile([P, PACK, P, PACK], BF16, name="w1_bf", align_bytes=64)
+        for h in range(2):
+            nc.scalar.copy(
+                w1_bf[:, :, h * 64 : (h + 1) * 64, :].rearrange("p t m j -> p m j t"),
+                w1_raw[h][:].rearrange("p j (m t) -> p m j t", t=PACK),
+            )
+        w1q = mx_tiles("w1q", H)
+        for t in range(PACK):
+            cols = slice(t * P, (t + 1) * P)
+            nc.vector.quantize_mx(
+                out=w1q[0][:, cols].bitcast(FP8X4), scales=w1q[1][:, cols], in_=w1_bf[:, t, :, :].rearrange("p m j -> p (m j)")
+            )
+        nc.vector.tensor_copy(xa[0][:], table_words[:].bitcast(U32).indirect(l_offs[:]))
+        nc.vector.tensor_copy(xb[0][:], table_words[:].bitcast(U32).indirect(l_two[:]))
+
+        everything = slice(0, S)
+        a_win, a_own = [], []
+        for t in range(PACK):
+            acc = psum.tile([P, S], F32, name="acc_a%d" % t, tag="low%d" % t)
+            product(acc[:], w1q, slice(t * P, (t + 1) * P), xa, everything)
+            win = keep.tile([P, S], F32, name="a_win%d" % t)
+            own = keep.tile([P, S], F32, name="a_own%d" % t)
+            nc.scalar.activation(win[:], acc[:], COPY, scale=ga_abs[:, t : t + 1])
+            nc.scalar.activation(own[:], acc[:], COPY, scale=ga_abs[:, t : t + 1])
+            a_win.append(win)
+            a_own.append(own)
+
+        w2_bf = keep.tile([P, PACK, P, PACK], BF16, name="w2_bf", align_bytes=64)
+        nc.scalar.copy(w2_bf[:].rearrange("p t m j -> p m j t"), w2_raw[:].rearrange("p j (m t) -> p m j t", t=PACK))
+        w2q = mx_tiles("w2q", H)
+
+        z = keep.tile([P, PACK, S], F32, name="z")
+        pending = []
+
+        def finish_z(t, d1, larger):
+            nc.vector.scalar_tensor_tensor(z[:, t, :], d1[:], 0.0, larger[:], ALU.max, ALU.subtract)
+
+        b_win, b_own = [], []
+        for t in range(PACK):
+            diffs = []
+            for name, offsets in (("d2", l2), ("d3", l3), ("d1", l1)):
+                d = keep.tile([P, S], F32, name="%s_%d" % (name, t))
+                for c in range(0, S, HALF):
+                    nc.vector.tensor_tensor(
+                        d[:, c : c + HALF], looked_up(a_win[t], offsets, c, HALF), a_own[t][:, c : c + HALF], ALU.subtract
+                    )
+                    if pending:
+                        finish_z(*pending.pop())
+                diffs.append(d)
+            larger = keep.tile([P, S], F32, name="larger%d" % t)
+            nc.vector.tensor_tensor(larger[:], diffs[0][:], diffs[1][:], ALU.max)
+            pending.append((t, diffs[2], larger))
+            if t == 0:
+                nc.vector.quantize_mx(
+                    out=w2q[0][:].bitcast(FP8X4), scales=w2q[1][:], in_=w2_bf[:].rearrange("p t m j -> p (t m j)")
+                )
+                for tb in range(PACK):
+                    acc = psum.tile([P, V], F32, name="acc_b%d" % tb, tag="high%d" % tb)
+                    product(acc[:], w2q, slice(tb * P, (tb + 1) * P), xb, everything)
+                    win = keep.tile([P, V], F32, name="b_win%d" % tb)
+                    own = keep.tile([P, V], F32, name="b_own%d" % tb)
+                    nc.scalar.activation(win[:], acc[:], COPY, scale=gb_34[:, tb : tb + 1])
+                    nc.scalar.activation(own[:], acc[:], COPY, scale=gb_one[:, tb : tb + 1])
+                    b_win.append(win)
+                    b_own.append(own)
+
+        z_bf = keep.tile([P, PACK, P, PACK], BF16, name="z_bf", align_bytes=64)
+        zq = mx_tiles("zq", S)
+        s_acc = [psum.tile([P, V], F32, name="acc_s%d" % t, tag="low%d" % t) for t in range(PACK)]
+        s_win = [keep.tile([P, V], F32, name="s_win%d" % t) for t in range(PACK)]
+        s_own = [keep.tile([P, V], F32, name="s_own%d" % t) for t in range(PACK)]
+
+        for first, count in B_CHUNKS:
+            cols = slice(first, first + count)
+            part = keep.tile([P, PACK, count], F32, name="part%d" % first)
+            z2 = keep.tile([P, PACK, count], F32, name="z2_%d" % first)
+            for t in range(PACK):
+                nc.vector.tensor_tensor(part[:, t, :], looked_up(b_win[t], l4, first, count), b_own[t][:, cols], ALU.subtract)
+                if pending:
+                    finish_z(*pending.pop())
+                    nc.scalar.copy(z_bf[:].rearrange("p t m j -> p m j t"), z[:].rearrange("p j (m t) -> p m j t", t=PACK))
+            for t in range(PACK):
+                nc.vector.tensor_tensor(z2[:, t, :], looked_up(b_win[t], l5, first, count), part[:, t, :], ALU.add)
+            if first == 0:
+                nc.vector.quantize_mx(out=zq[0][:].bitcast(FP8X4), scales=zq[1][:], in_=z_bf[:].rearrange("p t m j -> p (t m j)"))
+            z2_bf = keep.tile([P, count, PACK], BF16, name="z2_bf%d" % first, align_bytes=64)
+            nc.scalar.copy(z2_bf[:].rearrange("p (c i) j -> p c j i", i=4), z2[:].rearrange("p j (c i) -> p c j i", i=4))
+            z2q = mx_tiles("z2q%d" % first, count)
+            nc.vector.quantize_mx(out=z2q[0][:].bitcast(FP8X4), scales=z2q[1][:], in_=z2_bf[:].rearrange("p v j -> p (v j)"))
+            for t in range(PACK):
+                product(s_acc[t][:, cols], zq, slice(t * P, (t + 1) * P), z2q, slice(0, count))
+                nc.scalar.activation(s_win[t][:, cols], s_acc[t][:, cols], COPY, scale=0.0625)
+                nc.scalar.activation(s_own[t][:, cols], s_acc[t][:, cols], COPY, scale=0.75 * 0.0625)
+
+        out_rows = out.rearrange("(p t) v -> p t v", t=PACK)
+        waiting = []
+
+        def finish_out(t, cols, e6, e7):
+            res = keep.tile([P, HALF], F32, name="res%d_%d" % (t, cols.start))
+            nc.vector.tensor_tensor(res[:], e6[:], e7[:], ALU.max)
+            nc.sync.dma_start(out_rows[:, t, cols], res[:])
+
+        for t in range(PACK):
+            for c in range(0, V, HALF):
+                cols = slice(c, c + HALF)
+                e6 = keep.tile([P, HALF], F32, name="e6_%d_%d" % (t, c))
+                e7 = keep.tile([P, HALF], F32, name="e7_%d_%d" % (t, c))
+                nc.vector.tensor_tensor(e6[:], looked_up(s_win[t], l6, c, HALF), s_own[t][:, cols], ALU.subtract)
+                if waiting:
+                    finish_out(*waiting.pop())
+                nc.vector.tensor_tensor(e7[:], looked_up(s_win[t], l7, c, HALF), s_own[t][:, cols], ALU.subtract)
+                waiting.append((t, cols, e6, e7))
+        finish_out(*waiting.pop())

@@ -1,6 +1,7 @@
 from contextlib import ExitStack
 
 import concourse.mybir as mybir
+from concourse.masks import make_identity
 
 K, T, S, V, H = 512, 2048, 512, 512, 512
 FLOPS = 3 * 2 * 512 * 512 * 512
@@ -14,10 +15,12 @@ U8 = mybir.dt.uint8
 FP8X4 = mybir.dt.float8_e4m3fn_x4
 ALU = mybir.AluOpType
 COPY = mybir.ActivationFunctionType.Copy
+RELU = mybir.ActivationFunctionType.Relu
 
 P = 128
 PACK = 4
 HALF = 256
+WIDE = 1024
 B_CHUNKS = ((0, 256), (256, 128), (384, 128))
 
 
@@ -31,6 +34,7 @@ def tile_picked_kqmixlapover_none_p_kernel(
     nc = tc.nc
     with ExitStack() as ctx:
         keep = ctx.enter_context(tc.tile_pool(name="keep", bufs=1))
+        stage = ctx.enter_context(tc.tile_pool(name="stage", bufs=1))
         psum = ctx.enter_context(tc.psum_pool(name="psum", bufs=1))
 
         def load_list(name, src):
@@ -55,29 +59,30 @@ def tile_picked_kqmixlapover_none_p_kernel(
             )
 
         table_scales = keep.tile([P, T], U8, name="table_scales")
-        nc.vector.memset(table_scales[:].bitcast(I32), 0)
+        nc.gpsimd.memset(table_scales[:].bitcast(I32), 0)
         l_offs = load_list("offs", offs)
         l_two = load_list("two", two)
-        for q in range(4):
-            nc.scalar.dma_start(
-                table_scales[32 * q : 32 * q + 4, :].bitcast(I32), x_scales[0, 4 * q : 4 * q + 4, :].bitcast(I32)
-            )
         w1_rows = w1.rearrange("(p j) c -> p j c", j=PACK)
         w1_raw = []
         for h in range(2):
             raw = keep.tile([P, PACK, HALF], F32, name="w1_raw%d" % h)
             nc.sync.dma_start(raw[:], w1_rows[:, :, h * HALF : (h + 1) * HALF])
             w1_raw.append(raw)
+            if h == 0:
+                for q in range(4):
+                    nc.sync.dma_start(
+                        table_scales[32 * q : 32 * q + 4, :].bitcast(I32), x_scales[0, 4 * q : 4 * q + 4, :].bitcast(I32)
+                    )
         table_words = keep.tile([P, T], I32, name="table_words")
         nc.sync.dma_start(table_words[:], x_words[0].rearrange("p n t -> p (n t)").bitcast(I32))
         ga_t = keep.tile([P, PACK], F32, name="ga_t")
         gb_t = keep.tile([P, PACK], F32, name="gb_t")
-        nc.sync.dma_start(ga_t[:], ga.rearrange("(p t) o -> p (t o)", t=PACK))
-        nc.sync.dma_start(gb_t[:], gb.rearrange("(p t) o -> p (t o)", t=PACK))
+        nc.gpsimd.dma_start(ga_t[:], ga.rearrange("(p t) o -> p (t o)", t=PACK))
+        nc.gpsimd.dma_start(gb_t[:], gb.rearrange("(p t) o -> p (t o)", t=PACK))
         l1 = load_list("n1", n1)
         l2 = load_list("n2", n2)
         l3 = load_list("n3", n3)
-        w2_raw = keep.tile([P, PACK, H], F32, name="w2_raw")
+        w2_raw = stage.tile([P, PACK, H], F32, name="w2_raw", offset=0)
         nc.sync.dma_start(w2_raw[:], w2.rearrange("(p j) c -> p j c", j=PACK))
         l4 = load_list("n4", n4)
         l5 = load_list("n5", n5)
@@ -86,14 +91,24 @@ def tile_picked_kqmixlapover_none_p_kernel(
 
         sign = keep.tile([P, PACK], F32, name="sign")
         nonneg = keep.tile([P, PACK], F32, name="nonneg")
-        ga_abs = keep.tile([P, PACK], F32, name="ga_abs")
+        ga_abs = [
+            keep.tile([P, 2], F32, name="ga_abs0", tag="w2_bf", align_bytes=64),
+            keep.tile([P, 2], F32, name="ga_abs1"),
+        ]
+        ga_neg = keep.tile([P, PACK], F32, name="ga_neg")
+        ident = keep.tile([P, P], F32, name="ident")
         gb_one = keep.tile([P, PACK], F32, name="gb_one")
         gb_34 = keep.tile([P, PACK], F32, name="gb_34")
         nc.gpsimd.tensor_scalar(nonneg[:], ga_t[:], 0.0, 2.0, ALU.is_ge, ALU.mult)
         nc.gpsimd.tensor_scalar(sign[:], nonneg[:], 1.0, -1.0, ALU.mult, ALU.add)
-        nc.gpsimd.tensor_tensor(ga_abs[:], ga_t[:], sign[:], ALU.mult)
+        for h in range(2):
+            pair = slice(2 * h, 2 * h + 2)
+            nc.gpsimd.tensor_tensor(ga_abs[h][:], ga_t[:, pair], sign[:, pair], ALU.mult)
+            nc.gpsimd.tensor_scalar(ga_neg[:, pair], ga_abs[h][:], -1.0, 0.0, ALU.mult, ALU.add)
         nc.gpsimd.tensor_tensor(gb_one[:], gb_t[:], sign[:], ALU.mult)
         nc.gpsimd.tensor_scalar(gb_34[:], gb_one[:], 0.75, 0.0, ALU.mult, ALU.add)
+
+        make_identity(nc, ident[:])
 
         xa = mx_tiles("xa", S)
         xb = mx_tiles("xb", V)
@@ -112,52 +127,60 @@ def tile_picked_kqmixlapover_none_p_kernel(
             nc.vector.quantize_mx(
                 out=w1q[0][:, cols].bitcast(FP8X4), scales=w1q[1][:, cols], in_=w1_bf[:, t, :, :].rearrange("p m j -> p (m j)")
             )
-        nc.vector.tensor_copy(xa[0][:], table_words[:].bitcast(U32).indirect(l_offs[:]))
+        for c in range(0, S, HALF):
+            nc.vector.tensor_copy(
+                xa[0][:, c : c + HALF], table_words[:].bitcast(U32).indirect(l_offs[:, c // 16 : (c + HALF) // 16])
+            )
         nc.vector.tensor_copy(xb[0][:], table_words[:].bitcast(U32).indirect(l_two[:]))
 
         everything = slice(0, S)
-        a_win, a_own = [], []
+        a_pos, a_neg = [], []
         for t in range(PACK):
-            acc = psum.tile([P, S], F32, name="acc_a%d" % t, tag="low%d" % t)
-            product(acc[:], w1q, slice(t * P, (t + 1) * P), xa, everything)
-            win = keep.tile([P, S], F32, name="a_win%d" % t)
-            own = keep.tile([P, S], F32, name="a_own%d" % t)
-            nc.scalar.activation(win[:], acc[:], COPY, scale=ga_abs[:, t : t + 1])
-            nc.scalar.activation(own[:], acc[:], COPY, scale=ga_abs[:, t : t + 1])
-            a_win.append(win)
-            a_own.append(own)
+            acc = psum.tile([P, S], F32, name="acc_a%d" % t, tag="acc%d" % t)
+            width = HALF if t == 0 else S
+            for c in range(0, S, width):
+                product(acc[:, c : c + width], w1q, slice(t * P, (t + 1) * P), xa, slice(c, c + width))
+            pos = keep.tile([P, WIDE], F32, name="a_pos%d" % t)
+            if t < 2:
+                neg = keep.tile([P, WIDE], F32, name="a_neg%d" % t)
+            else:
+                neg = stage.tile([P, WIDE], F32, name="a_neg%d" % t, offset=(t - 2) * 4096)
+            nc.scalar.activation(neg[:, :S], acc[:], COPY, scale=ga_neg[:, t : t + 1])
+            nc.scalar.activation(pos[:, :S], acc[:], COPY, scale=ga_abs[t // 2][:, t % 2 : t % 2 + 1])
+            a_pos.append(pos)
+            a_neg.append(neg)
+            if t == 1:
+                w2_bf = keep.tile([P, PACK, P, PACK], BF16, name="w2_bf", tag="w2_bf", align_bytes=64)
+                nc.scalar.copy(w2_bf[:].rearrange("p t m j -> p m j t"), w2_raw[:].rearrange("p j (m t) -> p m j t", t=PACK))
 
-        w2_bf = keep.tile([P, PACK, P, PACK], BF16, name="w2_bf", align_bytes=64)
-        nc.scalar.copy(w2_bf[:].rearrange("p t m j -> p m j t"), w2_raw[:].rearrange("p j (m t) -> p m j t", t=PACK))
         w2q = mx_tiles("w2q", H)
 
-        z = keep.tile([P, PACK, S], F32, name="z")
-        pending = []
-
-        def finish_z(t, d1, larger):
-            nc.vector.scalar_tensor_tensor(z[:, t, :], d1[:], 0.0, larger[:], ALU.max, ALU.subtract)
-
+        turned = [psum.tile([P, PACK, P], F32, name="turned%d" % b, tag="turn%d" % b) for b in range(PACK)]
         b_win, b_own = [], []
         for t in range(PACK):
-            diffs = []
-            for name, offsets in (("d2", l2), ("d3", l3), ("d1", l1)):
-                d = keep.tile([P, S], F32, name="%s_%d" % (name, t))
-                for c in range(0, S, HALF):
-                    nc.vector.tensor_tensor(
-                        d[:, c : c + HALF], looked_up(a_win[t], offsets, c, HALF), a_own[t][:, c : c + HALF], ALU.subtract
+            neg2 = keep.tile([P, S], F32, name="neg2_%d" % t)
+            neg3 = keep.tile([P, S], F32, name="neg3_%d" % t)
+            rise = keep.tile([P, S], F32, name="rise%d" % t)
+            gain = keep.tile([P, S], F32, name="gain%d" % t)
+            least = keep.tile([P, S], F32, name="least%d" % t)
+            nc.vector.tensor_copy(neg2[:], a_neg[t][:].indirect(l2[:]))
+            nc.vector.tensor_copy(neg3[:], a_neg[t][:].indirect(l3[:]))
+            nc.vector.tensor_tensor(rise[:], a_pos[t][:].indirect(l1[:]), a_neg[t][:, :S], ALU.add)
+            nc.vector.tensor_tensor(least[:], neg2[:], neg3[:], ALU.min)
+            nc.scalar.activation(gain[:], rise[:], RELU)
+            for b in range(PACK):
+                cols = slice(b * P, (b + 1) * P)
+                terms = (a_pos[t], least, gain)
+                for i, term in enumerate(terms):
+                    nc.tensor.matmul(
+                        turned[b][:, t, :], term[:, cols], ident[:], start=(i == 0), stop=(i == len(terms) - 1), is_transpose=True
                     )
-                    if pending:
-                        finish_z(*pending.pop())
-                diffs.append(d)
-            larger = keep.tile([P, S], F32, name="larger%d" % t)
-            nc.vector.tensor_tensor(larger[:], diffs[0][:], diffs[1][:], ALU.max)
-            pending.append((t, diffs[2], larger))
-            if t == 0:
+            if t == 1:
                 nc.vector.quantize_mx(
                     out=w2q[0][:].bitcast(FP8X4), scales=w2q[1][:], in_=w2_bf[:].rearrange("p t m j -> p (t m j)")
                 )
                 for tb in range(PACK):
-                    acc = psum.tile([P, V], F32, name="acc_b%d" % tb, tag="high%d" % tb)
+                    acc = psum.tile([P, V], F32, name="acc_b%d" % tb, tag="acc%d" % tb)
                     product(acc[:], w2q, slice(tb * P, (tb + 1) * P), xb, everything)
                     win = keep.tile([P, V], F32, name="b_win%d" % tb)
                     own = keep.tile([P, V], F32, name="b_own%d" % tb)
@@ -166,50 +189,70 @@ def tile_picked_kqmixlapover_none_p_kernel(
                     b_win.append(win)
                     b_own.append(own)
 
-        z_bf = keep.tile([P, PACK, P, PACK], BF16, name="z_bf", align_bytes=64)
+        z_bf = keep.tile([P, PACK, P, PACK], BF16, name="z_bf", tag="reuse_z", align_bytes=64)
+        z_words = z_bf[:].bitcast(F32)
+        for hb in range(2):
+            pairs = []
+            for b in (2 * hb, 2 * hb + 1):
+                rows = keep.tile([P, 2, P, 2], BF16, name="z_rows%d" % b, tag="z2_bf0" if b == PACK - 1 else "z_rows%d" % b, align_bytes=64)
+                nc.scalar.copy(rows[:], turned[b][:].rearrange("r (u e) p -> r u p e", e=2))
+                pairs.append(rows[:].rearrange("r u p e -> r (u p e)").bitcast(F32))
+            back = psum.tile([P, 2, 2, P], F32, name="back%d" % hb, tag="turn%d" % (2 * hb))
+            for j in range(2):
+                for u in range(2):
+                    nc.tensor.transpose(back[:, j, u, :], pairs[j][:, u * P : (u + 1) * P], ident[:])
+            nc.scalar.copy(
+                z_words[:, :, 64 * hb : 64 * (hb + 1), :].rearrange("p t (j m) u -> p t j m u", j=2),
+                back[:].rearrange("p j u (m t) -> p t j m u", t=PACK),
+            )
         zq = mx_tiles("zq", S)
-        s_acc = [psum.tile([P, V], F32, name="acc_s%d" % t, tag="low%d" % t) for t in range(PACK)]
-        s_win = [keep.tile([P, V], F32, name="s_win%d" % t) for t in range(PACK)]
+        s_acc = [psum.tile([P, V], F32, name="acc_s%d" % t, tag="acc%d" % t) for t in range(PACK)]
+        s_win = [keep.tile([P, WIDE if t < PACK - 1 else V], F32, name="s_win%d" % t) for t in range(PACK)]
         s_own = [keep.tile([P, V], F32, name="s_own%d" % t) for t in range(PACK)]
+
+        def leave_psum(t, cols):
+            nc.scalar.activation(s_win[t][:, cols], s_acc[t][:, cols], COPY, scale=0.0625)
+            nc.scalar.activation(s_own[t][:, cols], s_acc[t][:, cols], COPY, scale=0.75 * 0.0625)
 
         for first, count in B_CHUNKS:
             cols = slice(first, first + count)
-            part = keep.tile([P, PACK, count], F32, name="part%d" % first)
-            z2 = keep.tile([P, PACK, count], F32, name="z2_%d" % first)
+            last = first + count == V
+            part = keep.tile([P, PACK, count], F32, name="part%d" % first, tag="reuse_z" if last else "part%d" % first, align_bytes=64)
+            z2 = keep.tile([P, PACK, count], F32, name="z2_%d" % first, tag="z2_bf0" if last else "z2_%d" % first, align_bytes=64)
             for t in range(PACK):
                 nc.vector.tensor_tensor(part[:, t, :], looked_up(b_win[t], l4, first, count), b_own[t][:, cols], ALU.subtract)
-                if pending:
-                    finish_z(*pending.pop())
-                    nc.scalar.copy(z_bf[:].rearrange("p t m j -> p m j t"), z[:].rearrange("p j (m t) -> p m j t", t=PACK))
             for t in range(PACK):
                 nc.vector.tensor_tensor(z2[:, t, :], looked_up(b_win[t], l5, first, count), part[:, t, :], ALU.add)
             if first == 0:
                 nc.vector.quantize_mx(out=zq[0][:].bitcast(FP8X4), scales=zq[1][:], in_=z_bf[:].rearrange("p t m j -> p (t m j)"))
-            z2_bf = keep.tile([P, count, PACK], BF16, name="z2_bf%d" % first, align_bytes=64)
+            z2_bf = keep.tile([P, count, PACK], BF16, name="z2_bf%d" % first, tag="z2_0" if first == HALF else "z2_bf%d" % first, align_bytes=64)
             nc.scalar.copy(z2_bf[:].rearrange("p (c i) j -> p c j i", i=4), z2[:].rearrange("p j (c i) -> p c j i", i=4))
             z2q = mx_tiles("z2q%d" % first, count)
             nc.vector.quantize_mx(out=z2q[0][:].bitcast(FP8X4), scales=z2q[1][:], in_=z2_bf[:].rearrange("p v j -> p (v j)"))
             for t in range(PACK):
                 product(s_acc[t][:, cols], zq, slice(t * P, (t + 1) * P), z2q, slice(0, count))
-                nc.scalar.activation(s_win[t][:, cols], s_acc[t][:, cols], COPY, scale=0.0625)
-                nc.scalar.activation(s_own[t][:, cols], s_acc[t][:, cols], COPY, scale=0.75 * 0.0625)
+                if t == 0:
+                    leave_psum(0, cols)
+            z2_last = z2
+        for t in range(1, PACK):
+            leave_psum(t, everything)
 
         out_rows = out.rearrange("(p t) v -> p t v", t=PACK)
         waiting = []
 
         def finish_out(t, cols, e6, e7):
-            res = keep.tile([P, HALF], F32, name="res%d_%d" % (t, cols.start))
+            res = keep.tile([P, cols.stop - cols.start], F32, name="res%d_%d" % (t, cols.start))
             nc.vector.tensor_tensor(res[:], e6[:], e7[:], ALU.max)
             nc.sync.dma_start(out_rows[:, t, cols], res[:])
 
         for t in range(PACK):
-            for c in range(0, V, HALF):
-                cols = slice(c, c + HALF)
-                e6 = keep.tile([P, HALF], F32, name="e6_%d_%d" % (t, c))
-                e7 = keep.tile([P, HALF], F32, name="e7_%d_%d" % (t, c))
-                nc.vector.tensor_tensor(e6[:], looked_up(s_win[t], l6, c, HALF), s_own[t][:, cols], ALU.subtract)
+            for c, width in ((0, V),) if t < PACK - 1 else B_CHUNKS:
+                cols = slice(c, c + width)
+                e6 = keep.tile([P, width], F32, name="e6_%d_%d" % (t, c))
+                e7 = keep.tile([P, width], F32, name="e7_%d_%d" % (t, c))
+                nc.vector.tensor_tensor(e6[:], looked_up(s_win[t], l6, c, width), s_own[t][:, cols], ALU.subtract)
                 if waiting:
                     finish_out(*waiting.pop())
-                nc.vector.tensor_tensor(e7[:], looked_up(s_win[t], l7, c, HALF), s_own[t][:, cols], ALU.subtract)
+                nc.vector.tensor_tensor(e7[:], looked_up(s_win[t], l7, c, width), s_own[t][:, cols], ALU.subtract)
                 waiting.append((t, cols, e6, e7))
         finish_out(*waiting.pop())

@@ -21,6 +21,7 @@ P = 128
 PACK = 4
 HALF = 256
 WIDE = 1024
+TURNED_TILES = 1
 B_CHUNKS = ((0, 256), (256, 128), (384, 128))
 
 
@@ -100,13 +101,12 @@ def tile_picked_kqmixlapover_none_p_kernel(
         gb_one = keep.tile([P, PACK], F32, name="gb_one")
         gb_34 = keep.tile([P, PACK], F32, name="gb_34")
         nc.gpsimd.tensor_scalar(nonneg[:], ga_t[:], 0.0, 2.0, ALU.is_ge, ALU.mult)
-        nc.gpsimd.tensor_scalar(sign[:], nonneg[:], 1.0, -1.0, ALU.mult, ALU.add)
+        nc.gpsimd.tensor_scalar(sign[:], nonneg[:], -1.0, 1.0, ALU.mult, ALU.add)
+        nc.gpsimd.tensor_tensor(ga_neg[:], ga_t[:], sign[:], ALU.mult)
         for h in range(2):
-            pair = slice(2 * h, 2 * h + 2)
-            nc.gpsimd.tensor_tensor(ga_abs[h][:], ga_t[:, pair], sign[:, pair], ALU.mult)
-            nc.gpsimd.tensor_scalar(ga_neg[:, pair], ga_abs[h][:], -1.0, 0.0, ALU.mult, ALU.add)
+            nc.gpsimd.tensor_scalar(ga_abs[h][:], ga_neg[:, 2 * h : 2 * h + 2], -1.0, 0.0, ALU.mult, ALU.add)
         nc.gpsimd.tensor_tensor(gb_one[:], gb_t[:], sign[:], ALU.mult)
-        nc.gpsimd.tensor_scalar(gb_34[:], gb_one[:], 0.75, 0.0, ALU.mult, ALU.add)
+        nc.gpsimd.tensor_scalar(gb_34[:], gb_one[:], -0.75, 0.0, ALU.mult, ALU.add)
 
         make_identity(nc, ident[:])
 
@@ -136,17 +136,21 @@ def tile_picked_kqmixlapover_none_p_kernel(
         everything = slice(0, S)
         a_pos, a_neg = [], []
         for t in range(PACK):
-            acc = psum.tile([P, S], F32, name="acc_a%d" % t, tag="acc%d" % t)
             width = HALF if t == 0 else S
+            accs = []
             for c in range(0, S, width):
-                product(acc[:, c : c + width], w1q, slice(t * P, (t + 1) * P), xa, slice(c, c + width))
+                acc = psum.tile([P, width], F32, name="acc_a%d_%d" % (t, c), tag="turn0" if c + width < S else "acc%d" % t)
+                product(acc[:], w1q, slice(t * P, (t + 1) * P), xa, slice(c, c + width))
+                accs.append((slice(c, c + width), acc))
             pos = keep.tile([P, WIDE], F32, name="a_pos%d" % t)
             if t < 2:
                 neg = keep.tile([P, WIDE], F32, name="a_neg%d" % t)
             else:
                 neg = stage.tile([P, WIDE], F32, name="a_neg%d" % t, offset=(t - 2) * 4096)
-            nc.scalar.activation(neg[:, :S], acc[:], COPY, scale=ga_neg[:, t : t + 1])
-            nc.scalar.activation(pos[:, :S], acc[:], COPY, scale=ga_abs[t // 2][:, t % 2 : t % 2 + 1])
+            for cols, acc in accs:
+                nc.scalar.activation(neg[:, cols], acc[:], COPY, scale=ga_neg[:, t : t + 1])
+            for cols, acc in accs:
+                nc.scalar.activation(pos[:, cols], acc[:], COPY, scale=ga_abs[t // 2][:, t % 2 : t % 2 + 1])
             a_pos.append(pos)
             a_neg.append(neg)
             if t == 1:
@@ -157,24 +161,35 @@ def tile_picked_kqmixlapover_none_p_kernel(
 
         turned = [psum.tile([P, PACK, P], F32, name="turned%d" % b, tag="turn%d" % b) for b in range(PACK)]
         b_win, b_own = [], []
+
+        def add_turned(acc, terms, cols):
+            for i, term in enumerate(terms):
+                nc.tensor.matmul(acc, term[:, cols], ident[:], start=(i == 0), stop=(i == len(terms) - 1), is_transpose=True)
+
+        def finish_z(t, neg2, drop, gain):
+            below = keep.tile([P, S], F32, name="below%d" % t)
+            nc.vector.tensor_scalar_min(below[:], drop[:], 0.0)
+            terms = (a_pos[t], neg2, gain, below)
+            for i, term in enumerate(terms):
+                for b in range(PACK):
+                    nc.tensor.matmul(
+                        turned[b][:, t, :], term[:, b * P : (b + 1) * P], ident[:],
+                        start=(i == 0), stop=(i == len(terms) - 1), is_transpose=True,
+                    )
+
+        pending = []
         for t in range(PACK):
             neg2 = keep.tile([P, S], F32, name="neg2_%d" % t)
-            neg3 = keep.tile([P, S], F32, name="neg3_%d" % t)
+            drop = keep.tile([P, S], F32, name="drop%d" % t)
             rise = keep.tile([P, S], F32, name="rise%d" % t)
             gain = keep.tile([P, S], F32, name="gain%d" % t)
-            least = keep.tile([P, S], F32, name="least%d" % t)
             nc.vector.tensor_copy(neg2[:], a_neg[t][:].indirect(l2[:]))
-            nc.vector.tensor_copy(neg3[:], a_neg[t][:].indirect(l3[:]))
+            if pending:
+                finish_z(*pending.pop())
             nc.vector.tensor_tensor(rise[:], a_pos[t][:].indirect(l1[:]), a_neg[t][:, :S], ALU.add)
-            nc.vector.tensor_tensor(least[:], neg2[:], neg3[:], ALU.min)
+            nc.vector.tensor_tensor(drop[:], a_neg[t][:].indirect(l3[:]), neg2[:], ALU.subtract)
             nc.scalar.activation(gain[:], rise[:], RELU)
-            for b in range(PACK):
-                cols = slice(b * P, (b + 1) * P)
-                terms = (a_pos[t], least, gain)
-                for i, term in enumerate(terms):
-                    nc.tensor.matmul(
-                        turned[b][:, t, :], term[:, cols], ident[:], start=(i == 0), stop=(i == len(terms) - 1), is_transpose=True
-                    )
+            pending.append((t, neg2, drop, gain))
             if t == 1:
                 nc.vector.quantize_mx(
                     out=w2q[0][:].bitcast(FP8X4), scales=w2q[1][:], in_=w2_bf[:].rearrange("p t m j -> p (t m j)")
@@ -188,6 +203,8 @@ def tile_picked_kqmixlapover_none_p_kernel(
                     nc.scalar.activation(own[:], acc[:], COPY, scale=gb_one[:, tb : tb + 1])
                     b_win.append(win)
                     b_own.append(own)
+
+        finish_z(*pending.pop())
 
         z_bf = keep.tile([P, PACK, P, PACK], BF16, name="z_bf", tag="reuse_z", align_bytes=64)
         z_words = z_bf[:].bitcast(F32)
@@ -210,34 +227,61 @@ def tile_picked_kqmixlapover_none_p_kernel(
         s_win = [keep.tile([P, WIDE if t < PACK - 1 else V], F32, name="s_win%d" % t) for t in range(PACK)]
         s_own = [keep.tile([P, V], F32, name="s_own%d" % t) for t in range(PACK)]
 
-        def leave_psum(t, cols):
-            nc.scalar.activation(s_win[t][:, cols], s_acc[t][:, cols], COPY, scale=0.0625)
-            nc.scalar.activation(s_own[t][:, cols], s_acc[t][:, cols], COPY, scale=0.75 * 0.0625)
+        def leave_psum(dst, t, cols, factor):
+            nc.scalar.activation(dst[t][:, cols], s_acc[t][:, cols], COPY, scale=factor * 0.0625)
 
-        for first, count in B_CHUNKS:
+        for n, (first, count) in enumerate(B_CHUNKS):
             cols = slice(first, first + count)
-            last = first + count == V
-            part = keep.tile([P, PACK, count], F32, name="part%d" % first, tag="reuse_z" if last else "part%d" % first, align_bytes=64)
-            z2 = keep.tile([P, PACK, count], F32, name="z2_%d" % first, tag="z2_bf0" if last else "z2_%d" % first, align_bytes=64)
+            if first % HALF == 0:
+                part = keep.tile([P, PACK, HALF], F32, name="part%d" % first)
+                for t in range(PACK):
+                    nc.vector.tensor_tensor(
+                        part[:, t, :], looked_up(b_win[t], l4, first, HALF), b_own[t][:, first : first + HALF], ALU.add
+                    )
+            z2 = keep.tile([P, PACK, count], F32, name="z2_%d" % first, tag=("z2_0", "reuse_z", "z2_bf0")[n], align_bytes=64)
+            within = slice(first % HALF, first % HALF + count)
             for t in range(PACK):
-                nc.vector.tensor_tensor(part[:, t, :], looked_up(b_win[t], l4, first, count), b_own[t][:, cols], ALU.subtract)
-            for t in range(PACK):
-                nc.vector.tensor_tensor(z2[:, t, :], looked_up(b_win[t], l5, first, count), part[:, t, :], ALU.add)
+                nc.vector.tensor_tensor(z2[:, t, :], looked_up(b_win[t], l5, first, count), part[:, t, within], ALU.add)
             if first == 0:
                 nc.vector.quantize_mx(out=zq[0][:].bitcast(FP8X4), scales=zq[1][:], in_=z_bf[:].rearrange("p t m j -> p (t m j)"))
             z2_bf = keep.tile([P, count, PACK], BF16, name="z2_bf%d" % first, tag="z2_0" if first == HALF else "z2_bf%d" % first, align_bytes=64)
-            nc.scalar.copy(z2_bf[:].rearrange("p (c i) j -> p c j i", i=4), z2[:].rearrange("p j (c i) -> p c j i", i=4))
+            weave = nc.vector.tensor_copy if first + count == V else nc.scalar.copy
+            weave(z2_bf[:].rearrange("p (c i) j -> p c j i", i=4), z2[:].rearrange("p j (c i) -> p c j i", i=4))
             z2q = mx_tiles("z2q%d" % first, count)
             nc.vector.quantize_mx(out=z2q[0][:].bitcast(FP8X4), scales=z2q[1][:], in_=z2_bf[:].rearrange("p v j -> p (v j)"))
             for t in range(PACK):
                 product(s_acc[t][:, cols], zq, slice(t * P, (t + 1) * P), z2q, slice(0, count))
                 if t == 0:
-                    leave_psum(0, cols)
-            z2_last = z2
-        for t in range(1, PACK):
-            leave_psum(t, everything)
+                    leave_psum(s_win, 0, cols, 1.0)
+        for t in range(1, TURNED_TILES):
+            leave_psum(s_win, t, everything, 1.0)
+        for t in range(TURNED_TILES):
+            leave_psum(s_own, t, everything, -0.75)
+        for t in range(TURNED_TILES, PACK):
+            leave_psum(s_win, t, everything, 1.0)
+            leave_psum(s_own, t, everything, 0.75)
 
         out_rows = out.rearrange("(p t) v -> p t v", t=PACK)
+        at6 = [keep.tile([P, V], F32, name="at6_%d" % t) for t in range(TURNED_TILES)]
+        for t in range(TURNED_TILES):
+            nc.vector.tensor_copy(at6[t][:], s_win[t][:].indirect(l6[:]))
+        for t in range(TURNED_TILES):
+            step = keep.tile([P, V], F32, name="step%d" % t)
+            lift = keep.tile([P, V], F32, name="lift%d" % t)
+            nc.vector.tensor_tensor(step[:], s_win[t][:].indirect(l7[:]), at6[t][:], ALU.subtract)
+            nc.scalar.activation(lift[:], step[:], RELU)
+            across = psum.tile([P, PACK, P], F32, name="across%d" % t, tag="turn%d" % (2 * t))
+            for b in range(PACK):
+                add_turned(across[:, b, :], (s_own[t], at6[t], lift), slice(b * P, (b + 1) * P))
+            across_sb = keep.tile([P, V], F32, name="across_sb%d" % t)
+            nc.scalar.copy(across_sb[:], across[:].rearrange("r b p -> r (b p)"))
+            upright = psum.tile([P, V], F32, name="upright%d" % t, tag="turn%d" % (2 * t + 1))
+            for b in range(PACK):
+                nc.tensor.transpose(upright[:, b * P : (b + 1) * P], across_sb[:, b * P : (b + 1) * P], ident[:])
+            res = keep.tile([P, V], F32, name="res%d" % t)
+            nc.scalar.copy(res[:], upright[:])
+            nc.scalar.dma_start(out_rows[:, t, :], res[:])
+
         waiting = []
 
         def finish_out(t, cols, e6, e7):
@@ -245,7 +289,7 @@ def tile_picked_kqmixlapover_none_p_kernel(
             nc.vector.tensor_tensor(res[:], e6[:], e7[:], ALU.max)
             nc.sync.dma_start(out_rows[:, t, cols], res[:])
 
-        for t in range(PACK):
+        for t in range(TURNED_TILES, PACK):
             for c, width in ((0, V),) if t < PACK - 1 else B_CHUNKS:
                 cols = slice(c, c + width)
                 e6 = keep.tile([P, width], F32, name="e6_%d_%d" % (t, c))

from contextlib import ExitStack

import concourse.mybir as mybir
from concourse.masks import make_identity

K, T, S, V, H = 512, 2048, 512, 512, 512
FLOPS = 3 * 2 * 512 * 512 * 512

F32 = mybir.dt.float32
BF16 = mybir.dt.bfloat16
I32 = mybir.dt.int32
U32 = mybir.dt.uint32
U16 = mybir.dt.uint16
U8 = mybir.dt.uint8
FP8X4 = mybir.dt.float8_e4m3fn_x4
ALU = mybir.AluOpType
COPY = mybir.ActivationFunctionType.Copy
RELU = mybir.ActivationFunctionType.Relu

P = 128
PACK = 4
HALF = 256
WIDE = 1024
TURNED_TILES = 1
B_CHUNKS = ((0, 256), (256, 128), (384, 128))


def looked_up(window, offsets, first, count):
    return window[:].indirect(offsets[:, first // 16 : (first + count) // 16])


def tile_picked_kqmixlapover_none_p_kernel(
    tc, x_words, x_scales, w1, w2, ga, gb, offs, two, n1, n2, n3, n4, n5, n6, n7, out
):
    nc = tc.nc
    with ExitStack() as ctx:
        keep = ctx.enter_context(tc.tile_pool(name="keep", bufs=1))
        stage = ctx.enter_context(tc.tile_pool(name="stage", bufs=1))
        psum = ctx.enter_context(tc.psum_pool(name="psum", bufs=1))

        def load_list(name, src):
            tile = keep.tile([P, S // 16], U16, name="list_" + name)
            nc.sync.dma_start(tile[:], src)
            return tile

        def mx_tiles(name, width):
            codes = keep.tile([P, width], U32, name=name + "_codes", align_bytes=64)
            scales = keep.tile([P, width], U8, name=name + "_scales", align_bytes=64)
            return codes, scales

        def product(acc, lhs, lhs_cols, rhs, rhs_cols):
            nc.tensor.matmul_mx(
                out=acc,
                lhsT=lhs[0][:, lhs_cols].bitcast(FP8X4),
                lhsT_scale=lhs[1][:, lhs_cols],
                rhs=rhs[0][:, rhs_cols].bitcast(FP8X4),
                rhs_scale=rhs[1][:, rhs_cols],
                start=True,
                stop=True,
            )

        table_scales = keep.tile([P, T], U8, name="table_scales")
        nc.gpsimd.memset(table_scales[:].bitcast(I32), 0)
        l_offs = load_list("offs", offs)
        l_two = load_list("two", two)
        w1_rows = w1.rearrange("(p j) c -> p j c", j=PACK)
        w1_raw = []
        for h in range(2):
            raw = keep.tile([P, PACK, HALF], F32, name="w1_raw%d" % h)
            nc.sync.dma_start(raw[:], w1_rows[:, :, h * HALF : (h + 1) * HALF])
            w1_raw.append(raw)
            if h == 0:
                for q in range(4):
                    nc.sync.dma_start(
                        table_scales[32 * q : 32 * q + 4, :].bitcast(I32), x_scales[0, 4 * q : 4 * q + 4, :].bitcast(I32)
                    )
        table_words = keep.tile([P, T], I32, name="table_words")
        nc.sync.dma_start(table_words[:], x_words[0].rearrange("p n t -> p (n t)").bitcast(I32))
        ga_t = keep.tile([P, PACK], F32, name="ga_t")
        gb_t = keep.tile([P, PACK], F32, name="gb_t")
        nc.gpsimd.dma_start(ga_t[:], ga.rearrange("(p t) o -> p (t o)", t=PACK))
        nc.gpsimd.dma_start(gb_t[:], gb.rearrange("(p t) o -> p (t o)", t=PACK))
        l1 = load_list("n1", n1)
        l2 = load_list("n2", n2)
        l3 = load_list("n3", n3)
        w2_raw = stage.tile([P, PACK, H], F32, name="w2_raw", offset=0)
        nc.sync.dma_start(w2_raw[:], w2.rearrange("(p j) c -> p j c", j=PACK))
        l4 = load_list("n4", n4)
        l5 = load_list("n5", n5)
        l6 = load_list("n6", n6)
        l7 = load_list("n7", n7)

        sign = keep.tile([P, PACK], F32, name="sign")
        nonneg = keep.tile([P, PACK], F32, name="nonneg")
        ga_abs = [
            keep.tile([P, 2], F32, name="ga_abs0", tag="w2_bf", align_bytes=64),
            keep.tile([P, 2], F32, name="ga_abs1"),
        ]
        ga_neg = keep.tile([P, PACK], F32, name="ga_neg")
        ident = keep.tile([P, P], F32, name="ident")
        gb_one = keep.tile([P, PACK], F32, name="gb_one")
        gb_34 = keep.tile([P, PACK], F32, name="gb_34")
        nc.gpsimd.tensor_scalar(nonneg[:], ga_t[:], 0.0, 2.0, ALU.is_ge, ALU.mult)
        nc.gpsimd.tensor_scalar(sign[:], nonneg[:], -1.0, 1.0, ALU.mult, ALU.add)
        nc.gpsimd.tensor_tensor(ga_neg[:], ga_t[:], sign[:], ALU.mult)
        for h in range(2):
            nc.gpsimd.tensor_scalar(ga_abs[h][:], ga_neg[:, 2 * h : 2 * h + 2], -1.0, 0.0, ALU.mult, ALU.add)
        nc.gpsimd.tensor_tensor(gb_one[:], gb_t[:], sign[:], ALU.mult)
        nc.gpsimd.tensor_scalar(gb_34[:], gb_one[:], -0.75, 0.0, ALU.mult, ALU.add)

        make_identity(nc, ident[:])

        xa = mx_tiles("xa", S)
        xb = mx_tiles("xb", V)
        nc.vector.tensor_copy(xa[1][:], table_scales[:].indirect(l_offs[:]))
        nc.vector.tensor_copy(xb[1][:], table_scales[:].indirect(l_two[:]))

        w1_bf = keep.tile([P, PACK, P, PACK], BF16, name="w1_bf", align_bytes=64)
        for h in range(2):
            nc.scalar.copy(
                w1_bf[:, :, h * 64 : (h + 1) * 64, :].rearrange("p t m j -> p m j t"),
                w1_raw[h][:].rearrange("p j (m t) -> p m j t", t=PACK),
            )
        w1q = mx_tiles("w1q", H)
        for t in range(PACK):
            cols = slice(t * P, (t + 1) * P)
            nc.vector.quantize_mx(
                out=w1q[0][:, cols].bitcast(FP8X4), scales=w1q[1][:, cols], in_=w1_bf[:, t, :, :].rearrange("p m j -> p (m j)")
            )
        for c in range(0, S, HALF):
            nc.vector.tensor_copy(
                xa[0][:, c : c + HALF], table_words[:].bitcast(U32).indirect(l_offs[:, c // 16 : (c + HALF) // 16])
            )
        nc.vector.tensor_copy(xb[0][:], table_words[:].bitcast(U32).indirect(l_two[:]))

        everything = slice(0, S)
        a_pos, a_neg = [], []
        for t in range(PACK):
            width = HALF if t == 0 else S
            accs = []
            for c in range(0, S, width):
                acc = psum.tile([P, width], F32, name="acc_a%d_%d" % (t, c), tag="turn0" if c + width < S else "acc%d" % t)
                product(acc[:], w1q, slice(t * P, (t + 1) * P), xa, slice(c, c + width))
                accs.append((slice(c, c + width), acc))
            pos = keep.tile([P, WIDE], F32, name="a_pos%d" % t)
            if t < 2:
                neg = keep.tile([P, WIDE], F32, name="a_neg%d" % t)
            else:
                neg = stage.tile([P, WIDE], F32, name="a_neg%d" % t, offset=(t - 2) * 4096)
            for cols, acc in accs:
                nc.scalar.activation(neg[:, cols], acc[:], COPY, scale=ga_neg[:, t : t + 1])
            for cols, acc in accs:
                nc.scalar.activation(pos[:, cols], acc[:], COPY, scale=ga_abs[t // 2][:, t % 2 : t % 2 + 1])
            a_pos.append(pos)
            a_neg.append(neg)
            if t == 1:
                w2_bf = keep.tile([P, PACK, P, PACK], BF16, name="w2_bf", tag="w2_bf", align_bytes=64)
                nc.scalar.copy(w2_bf[:].rearrange("p t m j -> p m j t"), w2_raw[:].rearrange("p j (m t) -> p m j t", t=PACK))

        w2q = mx_tiles("w2q", H)

        turned = [psum.tile([P, PACK, P], F32, name="turned%d" % b, tag="turn%d" % b) for b in range(PACK)]
        b_win, b_own = [], []

        def add_turned(acc, terms, cols):
            for i, term in enumerate(terms):
                nc.tensor.matmul(acc, term[:, cols], ident[:], start=(i == 0), stop=(i == len(terms) - 1), is_transpose=True)

        def finish_z(t, neg2, drop, gain):
            below = keep.tile([P, S], F32, name="below%d" % t)
            nc.vector.tensor_scalar_min(below[:], drop[:], 0.0)
            terms = (a_pos[t], neg2, gain, below)
            for i, term in enumerate(terms):
                for b in range(PACK):
                    nc.tensor.matmul(
                        turned[b][:, t, :], term[:, b * P : (b + 1) * P], ident[:],
                        start=(i == 0), stop=(i == len(terms) - 1), is_transpose=True,
                    )

        pending = []
        for t in range(PACK):
            neg2 = keep.tile([P, S], F32, name="neg2_%d" % t)
            drop = keep.tile([P, S], F32, name="drop%d" % t)
            rise = keep.tile([P, S], F32, name="rise%d" % t)
            gain = keep.tile([P, S], F32, name="gain%d" % t)
            nc.vector.tensor_copy(neg2[:], a_neg[t][:].indirect(l2[:]))
            if pending:
                finish_z(*pending.pop())
            nc.vector.tensor_tensor(rise[:], a_pos[t][:].indirect(l1[:]), a_neg[t][:, :S], ALU.add)
            nc.vector.tensor_tensor(drop[:], a_neg[t][:].indirect(l3[:]), neg2[:], ALU.subtract)
            nc.scalar.activation(gain[:], rise[:], RELU)
            pending.append((t, neg2, drop, gain))
            if t == 1:
                nc.vector.quantize_mx(
                    out=w2q[0][:].bitcast(FP8X4), scales=w2q[1][:], in_=w2_bf[:].rearrange("p t m j -> p (t m j)")
                )
                for tb in range(PACK):
                    acc = psum.tile([P, V], F32, name="acc_b%d" % tb, tag="acc%d" % tb)
                    product(acc[:], w2q, slice(tb * P, (tb + 1) * P), xb, everything)
                    win = keep.tile([P, V], F32, name="b_win%d" % tb)
                    own = keep.tile([P, V], F32, name="b_own%d" % tb)
                    nc.scalar.activation(win[:], acc[:], COPY, scale=gb_34[:, tb : tb + 1])
                    nc.scalar.activation(own[:], acc[:], COPY, scale=gb_one[:, tb : tb + 1])
                    b_win.append(win)
                    b_own.append(own)

        finish_z(*pending.pop())

        z_bf = keep.tile([P, PACK, P, PACK], BF16, name="z_bf", tag="reuse_z", align_bytes=64)
        z_words = z_bf[:].bitcast(F32)
        for hb in range(2):
            pairs = []
            for b in (2 * hb, 2 * hb + 1):
                rows = keep.tile([P, 2, P, 2], BF16, name="z_rows%d" % b, tag="z2_bf0" if b == PACK - 1 else "z_rows%d" % b, align_bytes=64)
                nc.scalar.copy(rows[:], turned[b][:].rearrange("r (u e) p -> r u p e", e=2))
                pairs.append(rows[:].rearrange("r u p e -> r (u p e)").bitcast(F32))
            back = psum.tile([P, 2, 2, P], F32, name="back%d" % hb, tag="turn%d" % (2 * hb))
            for j in range(2):
                for u in range(2):
                    nc.tensor.transpose(back[:, j, u, :], pairs[j][:, u * P : (u + 1) * P], ident[:])
            nc.scalar.copy(
                z_words[:, :, 64 * hb : 64 * (hb + 1), :].rearrange("p t (j m) u -> p t j m u", j=2),
                back[:].rearrange("p j u (m t) -> p t j m u", t=PACK),
            )
        zq = mx_tiles("zq", S)
        s_acc = [psum.tile([P, V], F32, name="acc_s%d" % t, tag="acc%d" % t) for t in range(PACK)]
        s_win = [keep.tile([P, WIDE if t < PACK - 1 else V], F32, name="s_win%d" % t) for t in range(PACK)]
        s_own = [keep.tile([P, V], F32, name="s_own%d" % t) for t in range(PACK)]

        def leave_psum(dst, t, cols, factor):
            nc.scalar.activation(dst[t][:, cols], s_acc[t][:, cols], COPY, scale=factor * 0.0625)

        for n, (first, count) in enumerate(B_CHUNKS):
            cols = slice(first, first + count)
            if first % HALF == 0:
                part = keep.tile([P, PACK, HALF], F32, name="part%d" % first)
                for t in range(PACK):
                    nc.vector.tensor_tensor(
                        part[:, t, :], looked_up(b_win[t], l4, first, HALF), b_own[t][:, first : first + HALF], ALU.add
                    )
            z2 = keep.tile([P, PACK, count], F32, name="z2_%d" % first, tag=("z2_0", "reuse_z", "z2_bf0")[n], align_bytes=64)
            within = slice(first % HALF, first % HALF + count)
            for t in range(PACK):
                nc.vector.tensor_tensor(z2[:, t, :], looked_up(b_win[t], l5, first, count), part[:, t, within], ALU.add)
            if first == 0:
                nc.vector.quantize_mx(out=zq[0][:].bitcast(FP8X4), scales=zq[1][:], in_=z_bf[:].rearrange("p t m j -> p (t m j)"))
            z2_bf = keep.tile([P, count, PACK], BF16, name="z2_bf%d" % first, tag="z2_0" if first == HALF else "z2_bf%d" % first, align_bytes=64)
            weave = nc.vector.tensor_copy if first + count == V else nc.scalar.copy
            weave(z2_bf[:].rearrange("p (c i) j -> p c j i", i=4), z2[:].rearrange("p j (c i) -> p c j i", i=4))
            z2q = mx_tiles("z2q%d" % first, count)
            nc.vector.quantize_mx(out=z2q[0][:].bitcast(FP8X4), scales=z2q[1][:], in_=z2_bf[:].rearrange("p v j -> p (v j)"))
            for t in range(PACK):
                product(s_acc[t][:, cols], zq, slice(t * P, (t + 1) * P), z2q, slice(0, count))
                if t == 0:
                    leave_psum(s_win, 0, cols, 1.0)
        for t in range(1, TURNED_TILES):
            leave_psum(s_win, t, everything, 1.0)
        for t in range(TURNED_TILES):
            leave_psum(s_own, t, everything, -0.75)
        for t in range(TURNED_TILES, PACK):
            leave_psum(s_win, t, everything, 1.0)
            leave_psum(s_own, t, everything, 0.75)

        out_rows = out.rearrange("(p t) v -> p t v", t=PACK)
        at6 = [keep.tile([P, V], F32, name="at6_%d" % t) for t in range(TURNED_TILES)]
        for t in range(TURNED_TILES):
            nc.vector.tensor_copy(at6[t][:], s_win[t][:].indirect(l6[:]))
        for t in range(TURNED_TILES):
            step = keep.tile([P, V], F32, name="step%d" % t)
            lift = keep.tile([P, V], F32, name="lift%d" % t)
            nc.vector.tensor_tensor(step[:], s_win[t][:].indirect(l7[:]), at6[t][:], ALU.subtract)
            nc.scalar.activation(lift[:], step[:], RELU)
            across = psum.tile([P, PACK, P], F32, name="across%d" % t, tag="turn%d" % (2 * t))
            for b in range(PACK):
                add_turned(across[:, b, :], (s_own[t], at6[t], lift), slice(b * P, (b + 1) * P))
            across_sb = keep.tile([P, V], F32, name="across_sb%d" % t)
            nc.scalar.copy(across_sb[:], across[:].rearrange("r b p -> r (b p)"))
            upright = psum.tile([P, V], F32, name="upright%d" % t, tag="turn%d" % (2 * t + 1))
            for b in range(PACK):
                nc.tensor.transpose(upright[:, b * P : (b + 1) * P], across_sb[:, b * P : (b + 1) * P], ident[:])
            res = keep.tile([P, V], F32, name="res%d" % t)
            nc.scalar.copy(res[:], upright[:])
            nc.scalar.dma_start(out_rows[:, t, :], res[:])

        waiting = []

        def finish_out(t, cols, e6, e7):
            res = keep.tile([P, cols.stop - cols.start], F32, name="res%d_%d" % (t, cols.start))
            nc.vector.tensor_tensor(res[:], e6[:], e7[:], ALU.max)
            nc.sync.dma_start(out_rows[:, t, cols], res[:])

        for t in range(TURNED_TILES, PACK):
            for c, width in ((0, V),) if t < PACK - 1 else B_CHUNKS:
                cols = slice(c, c + width)
                e6 = keep.tile([P, width], F32, name="e6_%d_%d" % (t, c))
                e7 = keep.tile([P, width], F32, name="e7_%d_%d" % (t, c))
                nc.vector.tensor_tensor(e6[:], looked_up(s_win[t], l6, c, width), s_own[t][:, cols], ALU.subtract)
                if waiting:
                    finish_out(*waiting.pop())
                nc.vector.tensor_tensor(e7[:], looked_up(s_win[t], l7, c, width), s_own[t][:, cols], ALU.subtract)
                waiting.append((t, cols, e6, e7))
        finish_out(*waiting.pop())
